import numpy as np
import ml_dtypes


def mxq(x, axis, fmt="e4m3"):
    dtype, down = {"e4m3": (ml_dtypes.float8_e4m3fn, 7), "e5m2": (ml_dtypes.float8_e5m2, 14)}[fmt]
    v = np.moveaxis(np.asarray(x, np.float32).astype(ml_dtypes.bfloat16).astype(np.float64), axis, -1)
    blocks = v.reshape(v.shape[:-1] + (-1, 32))
    amax = np.abs(blocks).max(-1, keepdims=True)
    byte = np.maximum(np.where(amax > 0, np.frexp(amax)[1] - 1 + 127, 0) - down, 1)
    scale = np.exp2(byte - 127.0)
    codes = (blocks / scale).astype(np.float32).astype(dtype).astype(np.float64)
    return np.moveaxis((codes * scale).reshape(v.shape), -1, axis)


WIDE = False


def mx_kscale(k):
    if not WIDE:
        return np.ones(k)
    levels = np.array([10, -10, 5, -5, 0])
    if k % 512:
        return np.exp2(np.random.permutation(np.resize(levels, k // 32))).repeat(32)
    a = np.empty((k // 512, 16))
    for p in range(k // 512):
        a[p, :8] = np.random.permutation(np.resize(levels, 8))
        for g in range(8):
            far = levels[np.abs(levels - a[p, g]) >= 10]
            a[p, g + 8] = far[np.random.randint(len(far))]
    return np.exp2(a.ravel()).repeat(32)


def f64(x):
    return np.asarray(x).astype(np.float64)


def striped(idx):
    return np.tile(idx.reshape(-1, 16).T, (8, 1)).astype(np.uint16)


def unstriped(offs):
    return offs[:16].T.reshape(-1).astype(np.int64)


def pack_weight(w):
    k, n = w.shape
    w = f64(np.asarray(w, np.float32).astype(ml_dtypes.bfloat16)).reshape(k // 32, 32, n)
    amax = np.abs(w).max(1)
    byte = np.clip(np.where(amax > 0, np.frexp(amax)[1] - 1 + 127 - 7, 1), 1, 254)
    scaled = (w * np.exp2(127.0 - byte)[:, None, :]).reshape(k, n).astype(np.float32)
    words = np.ascontiguousarray(scaled.reshape(k // 512, 128, 4, n).transpose(0, 1, 3, 2)).astype(ml_dtypes.float8_e4m3fn).view(np.uint8)
    return words, np.ascontiguousarray(byte.astype(np.uint8).reshape(k // 512, 16, n))


def unpack_weight(words, scales):
    g, p, n, _ = words.shape
    vals = np.ascontiguousarray(words).view(ml_dtypes.float8_e4m3fn).astype(np.float64) * np.repeat(np.exp2(scales.astype(np.float64) - 127.0), 8, axis=1)[..., None]
    return vals.transpose(0, 1, 3, 2).reshape(g * 512, n)


K, T, E, C, N = 1536, 768, 2, 256, 256


def by_expert(wq, xq):
    return np.concatenate([wq[e].T @ xq[:, e * C:(e + 1) * C] for e in range(E)], axis=1)


def setup_inputs():
    n = np.random.standard_normal
    s = mx_kscale(K)[:, None]
    packed = [pack_weight(m) for m in n((E, K, N)) / np.sqrt(K) / s[None]]
    return {
        "xT": (n((K, T)) * s).astype(np.float32),
        "w_words": np.stack([m[0] for m in packed]),
        "w_scales": np.stack([m[1] for m in packed]),
        "gate": np.tile(np.random.uniform(0.2, 1.0, E * C), (K, 1)).astype(np.float32),
        "offs": striped(np.random.permutation(T)[:E * C]),
    }


def reference(xT, w_words, w_scales, gate, offs):
    idx = unstriped(offs)
    w = np.stack([unpack_weight(w_words[e], w_scales[e]) for e in range(E)])
    xq = mxq(f64(gate) * f64(xT)[:, idx], 0, "e4m3")
    y = by_expert(w, xq)
    out = np.zeros((N, T))
    out[:, idx] = y
    return out

@@ -1,0 +1,144 @@
+from contextlib import ExitStack
+
+import concourse.mybir as mybir
+
+K, T, E, C, N = 1536, 768, 2, 256, 256
+S = E * C
+FLOPS = 2 * K * N * S
+P = 128
+PACK = 4
+K_PASS = P * PACK
+PASSES = K // K_PASS
+BLOCKS = N // P
+LIST_COLS = C // 16
+
+F32 = mybir.dt.float32
+BF16 = mybir.dt.bfloat16
+I32 = mybir.dt.int32
+U32 = mybir.dt.uint32
+U16 = mybir.dt.uint16
+U8 = mybir.dt.uint8
+FP8X4 = mybir.dt.float8_e4m3fn_x4
+MULT = mybir.AluOpType.mult
+
+
+def tile_moe_pre_lin_none_kernel(tc, xT, w_words, w_scales, gate, offs, out):
+    nc = tc.nc
+    with ExitStack() as ctx:
+        keep = ctx.enter_context(tc.tile_pool(name="keep", bufs=1))
+        psum = ctx.enter_context(tc.psum_pool(name="psum", bufs=1))
+
+        offsets = keep.tile([P, S // 16], U16, name="offsets")
+        gates = keep.tile([P, S], F32, name="gates")
+        x_rows = [[keep.tile([P, T], F32, name="x_%d_%d" % (a, t)) for t in range(PACK)] for a in range(PASSES)]
+        w_codes = [keep.tile([P, PASSES, N], U32, name="w_codes_%d" % e, align_bytes=64) for e in range(E)]
+        w_plane = keep.tile([P, E * PASSES, N], U8, name="w_plane", align_bytes=64)
+        windows = [keep.tile([P, T], F32, name="window_%d" % b) for b in range(BLOCKS)]
+
+        nc.vector.memset(w_plane[:].rearrange("p g n -> p (g n)").bitcast(I32), 0)
+        for b in range(BLOCKS):
+            nc.gpsimd.memset(windows[b][:], 0.0)
+
+        x_view = xT.rearrange("(a p t) c -> a t p c", p=P, t=PACK)
+        nc.sync.dma_start(offsets[:], offs)
+        nc.sync.dma_start(x_rows[0][0][:], x_view[0, 0])
+        nc.sync.dma_start(gates[:], gate[0:P, :])
+        for a in range(PASSES):
+            for t in range(PACK):
+                if (a, t) != (0, 0):
+                    nc.sync.dma_start(x_rows[a][t][:], x_view[a, t])
+
+        def load_words(e):
+            nc.sync.dma_start(w_codes[e][:].bitcast(I32), w_words[e].rearrange("a p n r -> p a (n r)").bitcast(I32))
+
+        load_words(0)
+        scale_rows = w_scales.rearrange("e a q n -> q (e a) n").bitcast(I32)
+        for quad in range(4):
+            nc.sync.dma_start(w_plane[32 * quad:32 * quad + 4].bitcast(I32), scale_rows[4 * quad:4 * quad + 4])
+        load_words(1)
+
+        gathered = {}
+        grouped = {}
+        x_codes = {}
+        x_plane = {}
+        sums = {}
+        results = {}
+
+        def gather(a, t, first, count):
+            key = (a, first)
+            if key not in gathered:
+                gathered[key] = keep.tile([P, PACK, count * C], F32, name="gathered_%d_%d" % key)
+            cols = slice(first * C, (first + count) * C)
+            entries = offsets[:, first * LIST_COLS:(first + count) * LIST_COLS]
+            nc.vector.tensor_tensor(gathered[key][:, t, :], x_rows[a][t][:].indirect(entries), gates[:, cols], MULT)
+
+        def interleave(a, first, count):
+            key = (a, first)
+            grouped[key] = keep.tile([P, count * C, PACK], BF16, name="grouped_%d_%d" % key, align_bytes=64)
+            nc.scalar.copy(grouped[key][:].rearrange("p (c i) t -> p c t i", i=4),
+                           gathered[key][:].rearrange("p t (c i) -> p c t i", i=4))
+
+        def quantise(a, first, count):
+            key = (a, first)
+            codes = keep.tile([P, count * C], U32, name="x_codes_%d_%d" % key, align_bytes=64)
+            plane = keep.tile([P, count * C], U8, name="x_plane_%d_%d" % key, align_bytes=64)
+            nc.vector.quantize_mx(out=codes[:].bitcast(FP8X4), scales=plane[:],
+                                  in_=grouped[key][:].rearrange("p c t -> p (c t)"))
+            for i in range(count):
+                x_codes[(a, first + i)] = codes[:, i * C:(i + 1) * C]
+                x_plane[(a, first + i)] = plane[:, i * C:(i + 1) * C]
+
+        def multiply(a, e):
+            for b in range(BLOCKS):
+                if a == 0:
+                    sums[(e, b)] = psum.tile([P, C], F32, name="sums_%d_%d" % (e, b))
+                cols = slice(b * P, (b + 1) * P)
+                nc.tensor.matmul_mx(out=sums[(e, b)][:],
+                                    lhsT=w_codes[e][:, a, cols].bitcast(FP8X4),
+                                    lhsT_scale=w_plane[:, e * PASSES + a, cols],
+                                    rhs=x_codes[(a, e)].bitcast(FP8X4),
+                                    rhs_scale=x_plane[(a, e)],
+                                    start=(a == 0), stop=(a == PASSES - 1))
+
+        def drain(e, b):
+            results[(e, b)] = keep.tile([P, C], F32, name="result_%d_%d" % (e, b))
+            nc.scalar.copy(results[(e, b)][:], sums[(e, b)][:])
+
+        def scatter(e, b):
+            entries = offsets[:, e * LIST_COLS:(e + 1) * LIST_COLS]
+            nc.vector.tensor_copy(windows[b][:].indirect(entries), results[(e, b)][:])
+
+        last = PASSES - 1
+        for t in range(PACK):
+            gather(0, t, 0, E)
+        interleave(0, 0, E)
+        for t in range(PACK):
+            gather(1, t, 0, E)
+        interleave(1, 0, E)
+        quantise(0, 0, E)
+        for t in range(PACK):
+            gather(last, t, 0, 1)
+        interleave(last, 0, 1)
+        quantise(1, 0, E)
+        for a in range(last):
+            multiply(a, 0)
+        for t in range(2):
+            gather(last, t, 1, 1)
+        quantise(last, 0, 1)
+        multiply(last, 0)
+        for b in range(BLOCKS):
+            drain(0, b)
+        for a in range(last):
+            multiply(a, 1)
+        for t in range(2, PACK):
+            gather(last, t, 1, 1)
+        interleave(last, 1, 1)
+        scatter(0, 0)
+        quantise(last, 1, 1)
+        multiply(last, 1)
+        for b in range(BLOCKS):
+            drain(1, b)
+        scatter(0, 1)
+        for b in range(BLOCKS):
+            scatter(1, b)
+            nc.sync.dma_start(out[b * P:(b + 1) * P, :], windows[b][:])

@@ -11,6 +11,7 @@ K_PASS = P * PACK
 PASSES = K // K_PASS
 BLOCKS = N // P
 LIST_COLS = C // 16
+HEAD = 128
 
 F32 = mybir.dt.float32
 BF16 = mybir.dt.bfloat16
@@ -40,9 +41,10 @@ def tile_moe_pre_lin_none_kernel(tc, xT, w_words, w_scales, gate, offs, out):
             nc.gpsimd.memset(windows[b][:], 0.0)
 
         x_view = xT.rearrange("(a p t) c -> a t p c", p=P, t=PACK)
+        nc.scalar.dma_start(x_rows[0][0][:], x_view[0, 0])
         nc.sync.dma_start(offsets[:], offs)
-        nc.sync.dma_start(x_rows[0][0][:], x_view[0, 0])
-        nc.sync.dma_start(gates[:], gate[0:P, :])
+        nc.sync.dma_start(gates[:, 0:HEAD], gate[0:P, 0:HEAD])
+        nc.sync.dma_start(gates[:, HEAD:], gate[0:P, HEAD:])
         for a in range(PASSES):
             for t in range(PACK):
                 if (a, t) != (0, 0):
@@ -57,33 +59,24 @@ def tile_moe_pre_lin_none_kernel(tc, xT, w_words, w_scales, gate, offs, out):
             nc.sync.dma_start(w_plane[32 * quad:32 * quad + 4].bitcast(I32), scale_rows[4 * quad:4 * quad + 4])
         load_words(1)
 
-        gathered = {}
-        grouped = {}
         x_codes = {}
         x_plane = {}
         sums = {}
-        results = {}
 
-        def gather(a, t, first, count):
-            key = (a, first)
-            if key not in gathered:
-                gathered[key] = keep.tile([P, PACK, count * C], F32, name="gathered_%d_%d" % key)
-            cols = slice(first * C, (first + count) * C)
-            entries = offsets[:, first * LIST_COLS:(first + count) * LIST_COLS]
-            nc.vector.tensor_tensor(gathered[key][:, t, :], x_rows[a][t][:].indirect(entries), gates[:, cols], MULT)
+        def gather(dst, a, t, base, width, first, stop):
+            entries = offsets[:, first // 16:stop // 16]
+            cols = slice(t * width + first - base, t * width + stop - base)
+            nc.vector.tensor_tensor(dst[:, cols], x_rows[a][t][:].indirect(entries), gates[:, first:stop], MULT)
 
-        def interleave(a, first, count):
-            key = (a, first)
-            grouped[key] = keep.tile([P, count * C, PACK], BF16, name="grouped_%d_%d" % key, align_bytes=64)
-            nc.scalar.copy(grouped[key][:].rearrange("p (c i) t -> p c t i", i=4),
-                           gathered[key][:].rearrange("p t (c i) -> p c t i", i=4))
+        def interleave(dst, src):
+            nc.scalar.copy(dst.rearrange("p (c i t) -> p c t i", i=4, t=PACK),
+                           src.rearrange("p (t c i) -> p c t i", i=4, t=PACK))
 
-        def quantise(a, first, count):
+        def quantise(src, a, first, count, tag=None):
             key = (a, first)
-            codes = keep.tile([P, count * C], U32, name="x_codes_%d_%d" % key, align_bytes=64)
+            codes = keep.tile([P, count * C], U32, name="x_codes_%d_%d" % key, tag=tag or "x_codes_%d_%d" % key, align_bytes=64)
             plane = keep.tile([P, count * C], U8, name="x_plane_%d_%d" % key, align_bytes=64)
-            nc.vector.quantize_mx(out=codes[:].bitcast(FP8X4), scales=plane[:],
-                                  in_=grouped[key][:].rearrange("p c t -> p (c t)"))
+            nc.vector.quantize_mx(out=codes[:].bitcast(FP8X4), scales=plane[:], in_=src)
             for i in range(count):
                 x_codes[(a, first + i)] = codes[:, i * C:(i + 1) * C]
                 x_plane[(a, first + i)] = plane[:, i * C:(i + 1) * C]
@@ -100,45 +93,55 @@ def tile_moe_pre_lin_none_kernel(tc, xT, w_words, w_scales, gate, offs, out):
                                     rhs_scale=x_plane[(a, e)],
                                     start=(a == 0), stop=(a == PASSES - 1))
 
-        def drain(e, b):
-            results[(e, b)] = keep.tile([P, C], F32, name="result_%d_%d" % (e, b))
-            nc.scalar.copy(results[(e, b)][:], sums[(e, b)][:])
-
-        def scatter(e, b):
+        def scatter(e, b, values):
             entries = offsets[:, e * LIST_COLS:(e + 1) * LIST_COLS]
-            nc.vector.tensor_copy(windows[b][:].indirect(entries), results[(e, b)][:])
+            nc.vector.tensor_copy(windows[b][:].indirect(entries), values)
 
         last = PASSES - 1
+        early = keep.tile([P, PACK * S], F32, name="early")
+        late = keep.tile([P, PACK * S + PACK * C], F32, name="late")
+        gathered = [early[:], late[:, 0:PACK * S]]
+        gathered_first = late[:, PACK * S:]
+        gathered_second = late[:, PACK * S - 2 * C:PACK * S + 2 * C]
+        grouped = []
+        for a in range(last):
+            for t in range(PACK):
+                if (a, t) == (0, 0):
+                    gather(gathered[a], a, t, 0, S, 0, HEAD)
+                    gather(gathered[a], a, t, 0, S, HEAD, S)
+                else:
+                    gather(gathered[a], a, t, 0, S, 0, S)
+            grouped.append(keep.tile([P, PACK * S], BF16, name="grouped_%d" % a, align_bytes=64))
+            interleave(grouped[a][:], gathered[a])
+            if a > 0:
+                quantise(grouped[a - 1][:], a - 1, 0, E)
+
         for t in range(PACK):
-            gather(0, t, 0, E)
-        interleave(0, 0, E)
-        for t in range(PACK):
-            gather(1, t, 0, E)
-        interleave(1, 0, E)
-        quantise(0, 0, E)
-        for t in range(PACK):
-            gather(last, t, 0, 1)
-        interleave(last, 0, 1)
-        quantise(1, 0, E)
+            gather(gathered_first, last, t, 0, C, 0, C)
+        grouped_first = keep.tile([P, PACK * C], BF16, name="grouped_first", align_bytes=64)
+        interleave(grouped_first[:], gathered_first)
+        quantise(grouped[1][:], 1, 0, E)
         for a in range(last):
             multiply(a, 0)
         for t in range(2):
-            gather(last, t, 1, 1)
-        quantise(last, 0, 1)
+            gather(gathered_second, last, t, C, C, C, S)
+        quantise(grouped_first[:], last, 0, 1, "handed_on")
         multiply(last, 0)
-        for b in range(BLOCKS):
-            drain(0, b)
+        results = keep.tile([P, E * BLOCKS - 1, C], F32, name="results")
+        nc.scalar.copy(results[:, 0, :], sums[(0, 0)][:])
         for a in range(last):
             multiply(a, 1)
         for t in range(2, PACK):
-            gather(last, t, 1, 1)
-        interleave(last, 1, 1)
-        scatter(0, 0)
-        quantise(last, 1, 1)
+            gather(gathered_second, last, t, C, C, C, S)
+        grouped_second = keep.tile([P, PACK * C], BF16, name="grouped_second", tag="handed_on", align_bytes=64)
+        interleave(grouped_second[:], gathered_second)
+        scatter(0, 0, results[:, 0, :])
+        nc.scalar.copy(gathered_second[:, 0:C], sums[(0, 1)][:])
+        quantise(grouped_second[:], last, 1, 1)
         multiply(last, 1)
         for b in range(BLOCKS):
-            drain(1, b)
-        scatter(0, 1)
+            nc.scalar.copy(results[:, 1 + b, :], sums[(1, b)][:])
+        scatter(0, 1, gathered_second[:, 0:C])
         for b in range(BLOCKS):
-            scatter(1, b)
+            scatter(1, b, results[:, 1 + b, :])
             nc.sync.dma_start(out[b * P:(b + 1) * P, :], windows[b][:])

@@ -31,7 +31,7 @@ def tile_moe_pre_lin_none_kernel(tc, xT, w_words, w_scales, gate, offs, out):
 
         offsets = keep.tile([P, S // 16], U16, name="offsets")
         gates = keep.tile([P, S], F32, name="gates")
-        x_rows = [[keep.tile([P, T], F32, name="x_%d_%d" % (a, t)) for t in range(PACK)] for a in range(PASSES)]
+        x_rows = [[keep.tile([P, T], F32, name="x_%d_%d" % (a, t), align_bytes=64) for t in range(PACK)] for a in range(PASSES)]
         w_codes = [keep.tile([P, PASSES, N], U32, name="w_codes_%d" % e, align_bytes=64) for e in range(E)]
         w_plane = keep.tile([P, E * PASSES, N], U8, name="w_plane", align_bytes=64)
         windows = [keep.tile([P, T], F32, name="window_%d" % b) for b in range(BLOCKS)]
@@ -72,26 +72,24 @@ def tile_moe_pre_lin_none_kernel(tc, xT, w_words, w_scales, gate, offs, out):
             nc.scalar.copy(dst.rearrange("p (c i t) -> p c t i", i=4, t=PACK),
                            src.rearrange("p (t c i) -> p c t i", i=4, t=PACK))
 
-        def quantise(src, a, first, count, tag=None):
-            key = (a, first)
-            codes = keep.tile([P, count * C], U32, name="x_codes_%d_%d" % key, tag=tag or "x_codes_%d_%d" % key, align_bytes=64)
-            plane = keep.tile([P, count * C], U8, name="x_plane_%d_%d" % key, align_bytes=64)
+        def quantise(src, keys, tag):
+            codes = keep.tile([P, len(keys) * C], U32, name="x_codes_" + tag, tag=tag, align_bytes=64)
+            plane = keep.tile([P, len(keys) * C], U8, name="x_plane_" + tag, align_bytes=64)
             nc.vector.quantize_mx(out=codes[:].bitcast(FP8X4), scales=plane[:], in_=src)
-            for i in range(count):
-                x_codes[(a, first + i)] = codes[:, i * C:(i + 1) * C]
-                x_plane[(a, first + i)] = plane[:, i * C:(i + 1) * C]
+            for i, key in enumerate(keys):
+                x_codes[key] = codes[:, i * C:(i + 1) * C]
+                x_plane[key] = plane[:, i * C:(i + 1) * C]
 
-        def multiply(a, e):
-            for b in range(BLOCKS):
-                if a == 0:
-                    sums[(e, b)] = psum.tile([P, C], F32, name="sums_%d_%d" % (e, b))
-                cols = slice(b * P, (b + 1) * P)
-                nc.tensor.matmul_mx(out=sums[(e, b)][:],
-                                    lhsT=w_codes[e][:, a, cols].bitcast(FP8X4),
-                                    lhsT_scale=w_plane[:, e * PASSES + a, cols],
-                                    rhs=x_codes[(a, e)].bitcast(FP8X4),
-                                    rhs_scale=x_plane[(a, e)],
-                                    start=(a == 0), stop=(a == PASSES - 1))
+        def multiply(a, e, b):
+            if a == 0:
+                sums[(e, b)] = psum.tile([P, C], F32, name="sums_%d_%d" % (e, b))
+            cols = slice(b * P, (b + 1) * P)
+            nc.tensor.matmul_mx(out=sums[(e, b)][:],
+                                lhsT=w_codes[e][:, a, cols].bitcast(FP8X4),
+                                lhsT_scale=w_plane[:, e * PASSES + a, cols],
+                                rhs=x_codes[(a, e)].bitcast(FP8X4),
+                                rhs_scale=x_plane[(a, e)],
+                                start=(a == 0), stop=(a == PASSES - 1))
 
         def scatter(e, b, values):
             entries = offsets[:, e * LIST_COLS:(e + 1) * LIST_COLS]
@@ -102,8 +100,7 @@ def tile_moe_pre_lin_none_kernel(tc, xT, w_words, w_scales, gate, offs, out):
         late = keep.tile([P, PACK * S + PACK * C], F32, name="late")
         gathered = [early[:], late[:, 0:PACK * S]]
         gathered_first = late[:, PACK * S:]
-        gathered_second = late[:, PACK * S - 2 * C:PACK * S + 2 * C]
-        grouped = []
+        gathered_second = late[:, PACK * S - C:PACK * S + (PACK - 1) * C]
         for a in range(last):
             for t in range(PACK):
                 if (a, t) == (0, 0):
@@ -111,34 +108,36 @@ def tile_moe_pre_lin_none_kernel(tc, xT, w_words, w_scales, gate, offs, out):
                     gather(gathered[a], a, t, 0, S, HEAD, S)
                 else:
                     gather(gathered[a], a, t, 0, S, 0, S)
-            grouped.append(keep.tile([P, PACK * S], BF16, name="grouped_%d" % a, align_bytes=64))
-            interleave(grouped[a][:], gathered[a])
-            if a > 0:
-                quantise(grouped[a - 1][:], a - 1, 0, E)
+        grouped = keep.tile([P, last * PACK * S], BF16, name="grouped", tag="x_1_1", align_bytes=64)
+        for a in range(last):
+            interleave(grouped[:, a * PACK * S:(a + 1) * PACK * S], gathered[a])
 
         for t in range(PACK):
             gather(gathered_first, last, t, 0, C, 0, C)
         grouped_first = keep.tile([P, PACK * C], BF16, name="grouped_first", align_bytes=64)
         interleave(grouped_first[:], gathered_first)
-        quantise(grouped[1][:], 1, 0, E)
-        for a in range(last):
-            multiply(a, 0)
-        for t in range(2):
-            gather(gathered_second, last, t, C, C, C, S)
-        quantise(grouped_first[:], last, 0, 1, "handed_on")
-        multiply(last, 0)
+        quantise(grouped[:], [(a, e) for a in range(last) for e in range(E)], "both")
+        for b in range(BLOCKS):
+            for a in range(last):
+                multiply(a, 0, b)
+        gather(gathered_second, last, 0, C, C, C, S)
+        quantise(grouped_first[:], [(last, 0)], "handed_on")
+        for b in range(BLOCKS):
+            multiply(last, 0, b)
         results = keep.tile([P, E * BLOCKS - 1, C], F32, name="results")
         nc.scalar.copy(results[:, 0, :], sums[(0, 0)][:])
-        for a in range(last):
-            multiply(a, 1)
-        for t in range(2, PACK):
+        for b in range(BLOCKS):
+            for a in range(last):
+                multiply(a, 1, b)
+        for t in range(1, PACK):
             gather(gathered_second, last, t, C, C, C, S)
         grouped_second = keep.tile([P, PACK * C], BF16, name="grouped_second", tag="handed_on", align_bytes=64)
         interleave(grouped_second[:], gathered_second)
         scatter(0, 0, results[:, 0, :])
         nc.scalar.copy(gathered_second[:, 0:C], sums[(0, 1)][:])
-        quantise(grouped_second[:], last, 1, 1)
-        multiply(last, 1)
+        quantise(grouped_second[:], [(last, 1)], "second")
+        for b in range(BLOCKS):
+            multiply(last, 1, b)
         for b in range(BLOCKS):
             nc.scalar.copy(results[:, 1 + b, :], sums[(1, b)][:])
         scatter(0, 1, gathered_second[:, 0:C])

@@ -7,10 +7,12 @@ S = E * C
 FLOPS = 2 * K * N * S
 P = 128
 PACK = 4
-K_PASS = P * PACK
-PASSES = K // K_PASS
+PASSES = K // (P * PACK)
+LAST = PASSES - 1
 BLOCKS = N // P
-LIST_COLS = C // 16
+STRIPE = 16
+QUADRANTS = 4
+LINE = 4
 HEAD = 128
 
 F32 = mybir.dt.float32
@@ -29,21 +31,22 @@ def tile_moe_pre_lin_none_kernel(tc, xT, w_words, w_scales, gate, offs, out):
         keep = ctx.enter_context(tc.tile_pool(name="keep", bufs=1))
         psum = ctx.enter_context(tc.psum_pool(name="psum", bufs=1))
 
-        offsets = keep.tile([P, S // 16], U16, name="offsets")
+        offsets = keep.tile([P, S // STRIPE], U16, name="offsets")
         gates = keep.tile([P, S], F32, name="gates")
-        x_rows = [[keep.tile([P, T], F32, name="x_%d_%d" % (a, t), align_bytes=64) for t in range(PACK)] for a in range(PASSES)]
+        x_rows = [[keep.tile([P, T], F32, name="x_%d_%d" % (a, t), align_bytes=64) for t in range(PACK)]
+                  for a in range(PASSES)]
         w_codes = [keep.tile([P, PASSES, N], U32, name="w_codes_%d" % e, align_bytes=64) for e in range(E)]
-        w_plane = keep.tile([P, E * PASSES, N], U8, name="w_plane", align_bytes=64)
+        w_scale = keep.tile([P, E * PASSES, N], U8, name="w_plane", align_bytes=64)
         windows = [keep.tile([P, T], F32, name="window_%d" % b) for b in range(BLOCKS)]
 
-        nc.vector.memset(w_plane[:].rearrange("p g n -> p (g n)").bitcast(I32), 0)
+        nc.vector.memset(w_scale[:].rearrange("p g n -> p (g n)").bitcast(I32), 0)
         for b in range(BLOCKS):
             nc.gpsimd.memset(windows[b][:], 0.0)
 
         x_view = xT.rearrange("(a p t) c -> a t p c", p=P, t=PACK)
-        nc.scalar.dma_start(x_rows[0][0][:], x_view[0, 0])
+        nc.sync.dma_start(x_rows[0][0][:], x_view[0, 0])
+        nc.scalar.dma_start(gates[:, 0:HEAD], gate[0:P, 0:HEAD])
         nc.sync.dma_start(offsets[:], offs)
-        nc.sync.dma_start(gates[:, 0:HEAD], gate[0:P, 0:HEAD])
         nc.sync.dma_start(gates[:, HEAD:], gate[0:P, HEAD:])
         for a in range(PASSES):
             for t in range(PACK):
@@ -55,30 +58,30 @@ def tile_moe_pre_lin_none_kernel(tc, xT, w_words, w_scales, gate, offs, out):
 
         load_words(0)
         scale_rows = w_scales.rearrange("e a q n -> q (e a) n").bitcast(I32)
-        for quad in range(4):
-            nc.sync.dma_start(w_plane[32 * quad:32 * quad + 4].bitcast(I32), scale_rows[4 * quad:4 * quad + 4])
+        for quad in range(QUADRANTS):
+            nc.sync.dma_start(w_scale[32 * quad:32 * quad + 4].bitcast(I32), scale_rows[4 * quad:4 * quad + 4])
         load_words(1)
 
         x_codes = {}
-        x_plane = {}
+        x_scale = {}
         sums = {}
 
         def gather(dst, a, t, base, width, first, stop):
-            entries = offsets[:, first // 16:stop // 16]
+            entries = offsets[:, first // STRIPE:stop // STRIPE]
             cols = slice(t * width + first - base, t * width + stop - base)
             nc.vector.tensor_tensor(dst[:, cols], x_rows[a][t][:].indirect(entries), gates[:, first:stop], MULT)
 
         def interleave(dst, src):
-            nc.scalar.copy(dst.rearrange("p (c i t) -> p c t i", i=4, t=PACK),
-                           src.rearrange("p (t c i) -> p c t i", i=4, t=PACK))
+            nc.scalar.copy(dst.rearrange("p (c i t) -> p c t i", i=LINE, t=PACK),
+                           src.rearrange("p (t c i) -> p c t i", i=LINE, t=PACK))
 
         def quantise(src, keys, tag):
             codes = keep.tile([P, len(keys) * C], U32, name="x_codes_" + tag, tag=tag, align_bytes=64)
-            plane = keep.tile([P, len(keys) * C], U8, name="x_plane_" + tag, align_bytes=64)
-            nc.vector.quantize_mx(out=codes[:].bitcast(FP8X4), scales=plane[:], in_=src)
+            scale = keep.tile([P, len(keys) * C], U8, name="x_plane_" + tag, align_bytes=64)
+            nc.vector.quantize_mx(out=codes[:].bitcast(FP8X4), scales=scale[:], in_=src)
             for i, key in enumerate(keys):
                 x_codes[key] = codes[:, i * C:(i + 1) * C]
-                x_plane[key] = plane[:, i * C:(i + 1) * C]
+                x_scale[key] = scale[:, i * C:(i + 1) * C]
 
         def multiply(a, e, b):
             if a == 0:
@@ -86,58 +89,59 @@ def tile_moe_pre_lin_none_kernel(tc, xT, w_words, w_scales, gate, offs, out):
             cols = slice(b * P, (b + 1) * P)
             nc.tensor.matmul_mx(out=sums[(e, b)][:],
                                 lhsT=w_codes[e][:, a, cols].bitcast(FP8X4),
-                                lhsT_scale=w_plane[:, e * PASSES + a, cols],
+                                lhsT_scale=w_scale[:, e * PASSES + a, cols],
                                 rhs=x_codes[(a, e)].bitcast(FP8X4),
-                                rhs_scale=x_plane[(a, e)],
-                                start=(a == 0), stop=(a == PASSES - 1))
+                                rhs_scale=x_scale[(a, e)],
+                                start=(a == 0), stop=(a == LAST))
 
         def scatter(e, b, values):
-            entries = offsets[:, e * LIST_COLS:(e + 1) * LIST_COLS]
+            entries = offsets[:, e * C // STRIPE:(e + 1) * C // STRIPE]
             nc.vector.tensor_copy(windows[b][:].indirect(entries), values)
 
-        last = PASSES - 1
         early = keep.tile([P, PACK * S], F32, name="early")
         late = keep.tile([P, PACK * S + PACK * C], F32, name="late")
         gathered = [early[:], late[:, 0:PACK * S]]
         gathered_first = late[:, PACK * S:]
         gathered_second = late[:, PACK * S - C:PACK * S + (PACK - 1) * C]
-        for a in range(last):
+
+        for a in range(LAST):
             for t in range(PACK):
                 if (a, t) == (0, 0):
                     gather(gathered[a], a, t, 0, S, 0, HEAD)
                     gather(gathered[a], a, t, 0, S, HEAD, S)
                 else:
                     gather(gathered[a], a, t, 0, S, 0, S)
-        grouped = keep.tile([P, last * PACK * S], BF16, name="grouped", tag="x_1_1", align_bytes=64)
-        for a in range(last):
+        grouped = keep.tile([P, LAST * PACK * S], BF16, name="grouped", tag="x_1_1", align_bytes=64)
+        for a in range(LAST):
             interleave(grouped[:, a * PACK * S:(a + 1) * PACK * S], gathered[a])
 
         for t in range(PACK):
-            gather(gathered_first, last, t, 0, C, 0, C)
+            gather(gathered_first, LAST, t, 0, C, 0, C)
         grouped_first = keep.tile([P, PACK * C], BF16, name="grouped_first", align_bytes=64)
         interleave(grouped_first[:], gathered_first)
-        quantise(grouped[:], [(a, e) for a in range(last) for e in range(E)], "both")
+        quantise(grouped[:], [(a, e) for a in range(LAST) for e in range(E)], "both")
         for b in range(BLOCKS):
-            for a in range(last):
+            for a in range(LAST):
                 multiply(a, 0, b)
-        gather(gathered_second, last, 0, C, C, C, S)
-        quantise(grouped_first[:], [(last, 0)], "handed_on")
+        gather(gathered_second, LAST, 0, C, C, C, S)
+        quantise(grouped_first[:], [(LAST, 0)], "handed_on")
         for b in range(BLOCKS):
-            multiply(last, 0, b)
+            multiply(LAST, 0, b)
         results = keep.tile([P, E * BLOCKS - 1, C], F32, name="results")
         nc.scalar.copy(results[:, 0, :], sums[(0, 0)][:])
+
         for b in range(BLOCKS):
-            for a in range(last):
+            for a in range(LAST):
                 multiply(a, 1, b)
         for t in range(1, PACK):
-            gather(gathered_second, last, t, C, C, C, S)
+            gather(gathered_second, LAST, t, C, C, C, S)
         grouped_second = keep.tile([P, PACK * C], BF16, name="grouped_second", tag="handed_on", align_bytes=64)
         interleave(grouped_second[:], gathered_second)
         scatter(0, 0, results[:, 0, :])
         nc.scalar.copy(gathered_second[:, 0:C], sums[(0, 1)][:])
-        quantise(grouped_second[:], [(last, 1)], "second")
+        quantise(grouped_second[:], [(LAST, 1)], "second")
         for b in range(BLOCKS):
-            multiply(last, 1, b)
+            multiply(LAST, 1, b)
         for b in range(BLOCKS):
             nc.scalar.copy(results[:, 1 + b, :], sums[(1, b)][:])
         scatter(0, 1, gathered_second[:, 0:C])

from contextlib import ExitStack

import concourse.mybir as mybir

K, T, E, C, N = 1536, 768, 2, 256, 256
S = E * C
FLOPS = 2 * K * N * S
P = 128
PACK = 4
PASSES = K // (P * PACK)
LAST = PASSES - 1
BLOCKS = N // P
STRIPE = 16
QUADRANTS = 4
LINE = 4
HEAD = 128

F32 = mybir.dt.float32
BF16 = mybir.dt.bfloat16
I32 = mybir.dt.int32
U32 = mybir.dt.uint32
U16 = mybir.dt.uint16
U8 = mybir.dt.uint8
FP8X4 = mybir.dt.float8_e4m3fn_x4
MULT = mybir.AluOpType.mult


def tile_moe_pre_lin_none_kernel(tc, xT, w_words, w_scales, gate, offs, out):
    nc = tc.nc
    with ExitStack() as ctx:
        keep = ctx.enter_context(tc.tile_pool(name="keep", bufs=1))
        psum = ctx.enter_context(tc.psum_pool(name="psum", bufs=1))

        offsets = keep.tile([P, S // STRIPE], U16, name="offsets")
        gates = keep.tile([P, S], F32, name="gates")
        x_rows = [[keep.tile([P, T], F32, name="x_%d_%d" % (a, t), align_bytes=64) for t in range(PACK)]
                  for a in range(PASSES)]
        w_codes = [keep.tile([P, PASSES, N], U32, name="w_codes_%d" % e, align_bytes=64) for e in range(E)]
        w_scale = keep.tile([P, E * PASSES, N], U8, name="w_plane", align_bytes=64)
        windows = [keep.tile([P, T], F32, name="window_%d" % b) for b in range(BLOCKS)]

        nc.vector.memset(w_scale[:].rearrange("p g n -> p (g n)").bitcast(I32), 0)
        for b in range(BLOCKS):
            nc.gpsimd.memset(windows[b][:], 0.0)

        x_view = xT.rearrange("(a p t) c -> a t p c", p=P, t=PACK)
        nc.sync.dma_start(x_rows[0][0][:], x_view[0, 0])
        nc.scalar.dma_start(gates[:, 0:HEAD], gate[0:P, 0:HEAD])
        nc.sync.dma_start(offsets[:], offs)
        nc.sync.dma_start(gates[:, HEAD:], gate[0:P, HEAD:])
        for a in range(PASSES):
            for t in range(PACK):
                if (a, t) != (0, 0):
                    nc.sync.dma_start(x_rows[a][t][:], x_view[a, t])

        def load_words(e):
            nc.sync.dma_start(w_codes[e][:].bitcast(I32), w_words[e].rearrange("a p n r -> p a (n r)").bitcast(I32))

        load_words(0)
        scale_rows = w_scales.rearrange("e a q n -> q (e a) n").bitcast(I32)
        for quad in range(QUADRANTS):
            nc.sync.dma_start(w_scale[32 * quad:32 * quad + 4].bitcast(I32), scale_rows[4 * quad:4 * quad + 4])
        load_words(1)

        x_codes = {}
        x_scale = {}
        sums = {}

        def gather(dst, a, t, base, width, first, stop):
            entries = offsets[:, first // STRIPE:stop // STRIPE]
            cols = slice(t * width + first - base, t * width + stop - base)
            nc.vector.tensor_tensor(dst[:, cols], x_rows[a][t][:].indirect(entries), gates[:, first:stop], MULT)

        def interleave(dst, src):
            nc.scalar.copy(dst.rearrange("p (c i t) -> p c t i", i=LINE, t=PACK),
                           src.rearrange("p (t c i) -> p c t i", i=LINE, t=PACK))

        def quantise(src, keys, tag):
            codes = keep.tile([P, len(keys) * C], U32, name="x_codes_" + tag, tag=tag, align_bytes=64)
            scale = keep.tile([P, len(keys) * C], U8, name="x_plane_" + tag, align_bytes=64)
            nc.vector.quantize_mx(out=codes[:].bitcast(FP8X4), scales=scale[:], in_=src)
            for i, key in enumerate(keys):
                x_codes[key] = codes[:, i * C:(i + 1) * C]
                x_scale[key] = scale[:, i * C:(i + 1) * C]

        def multiply(a, e, b):
            if a == 0:
                sums[(e, b)] = psum.tile([P, C], F32, name="sums_%d_%d" % (e, b))
            cols = slice(b * P, (b + 1) * P)
            nc.tensor.matmul_mx(out=sums[(e, b)][:],
                                lhsT=w_codes[e][:, a, cols].bitcast(FP8X4),
                                lhsT_scale=w_scale[:, e * PASSES + a, cols],
                                rhs=x_codes[(a, e)].bitcast(FP8X4),
                                rhs_scale=x_scale[(a, e)],
                                start=(a == 0), stop=(a == LAST))

        def scatter(e, b, values):
            entries = offsets[:, e * C // STRIPE:(e + 1) * C // STRIPE]
            nc.vector.tensor_copy(windows[b][:].indirect(entries), values)

        early = keep.tile([P, PACK * S], F32, name="early")
        late = keep.tile([P, PACK * S + PACK * C], F32, name="late")
        gathered = [early[:], late[:, 0:PACK * S]]
        gathered_first = late[:, PACK * S:]
        gathered_second = late[:, PACK * S - C:PACK * S + (PACK - 1) * C]

        for a in range(LAST):
            for t in range(PACK):
                if (a, t) == (0, 0):
                    gather(gathered[a], a, t, 0, S, 0, HEAD)
                    gather(gathered[a], a, t, 0, S, HEAD, S)
                else:
                    gather(gathered[a], a, t, 0, S, 0, S)
        grouped = keep.tile([P, LAST * PACK * S], BF16, name="grouped", tag="x_1_1", align_bytes=64)
        for a in range(LAST):
            interleave(grouped[:, a * PACK * S:(a + 1) * PACK * S], gathered[a])

        for t in range(PACK):
            gather(gathered_first, LAST, t, 0, C, 0, C)
        grouped_first = keep.tile([P, PACK * C], BF16, name="grouped_first", align_bytes=64)
        interleave(grouped_first[:], gathered_first)
        quantise(grouped[:], [(a, e) for a in range(LAST) for e in range(E)], "both")
        for b in range(BLOCKS):
            for a in range(LAST):
                multiply(a, 0, b)
        gather(gathered_second, LAST, 0, C, C, C, S)
        quantise(grouped_first[:], [(LAST, 0)], "handed_on")
        for b in range(BLOCKS):
            multiply(LAST, 0, b)
        results = keep.tile([P, E * BLOCKS - 1, C], F32, name="results")
        nc.scalar.copy(results[:, 0, :], sums[(0, 0)][:])

        for b in range(BLOCKS):
            for a in range(LAST):
                multiply(a, 1, b)
        for t in range(1, PACK):
            gather(gathered_second, LAST, t, C, C, C, S)
        grouped_second = keep.tile([P, PACK * C], BF16, name="grouped_second", tag="handed_on", align_bytes=64)
        interleave(grouped_second[:], gathered_second)
        scatter(0, 0, results[:, 0, :])
        nc.scalar.copy(gathered_second[:, 0:C], sums[(0, 1)][:])
        quantise(grouped_second[:], [(LAST, 1)], "second")
        for b in range(BLOCKS):
            multiply(LAST, 1, b)
        for b in range(BLOCKS):
            nc.scalar.copy(results[:, 1 + b, :], sums[(1, b)][:])
        scatter(0, 1, gathered_second[:, 0:C])
        for b in range(BLOCKS):
            scatter(1, b, results[:, 1 + b, :])
            nc.sync.dma_start(out[b * P:(b + 1) * P, :], windows[b][:])
